import numpy as np
import ml_dtypes


def mxq(x, axis, fmt="e4m3"):
    dtype, down = {"e4m3": (ml_dtypes.float8_e4m3fn, 7), "e5m2": (ml_dtypes.float8_e5m2, 14)}[fmt]
    v = np.moveaxis(np.asarray(x, np.float32).astype(ml_dtypes.bfloat16).astype(np.float64), axis, -1)
    blocks = v.reshape(v.shape[:-1] + (-1, 32))
    amax = np.abs(blocks).max(-1, keepdims=True)
    byte = np.maximum(np.where(amax > 0, np.frexp(amax)[1] - 1 + 127, 0) - down, 1)
    scale = np.exp2(byte - 127.0)
    codes = (blocks / scale).astype(np.float32).astype(dtype).astype(np.float64)
    return np.moveaxis((codes * scale).reshape(v.shape), -1, axis)


WIDE = False


def mx_kscale(k):
    if not WIDE:
        return np.ones(k)
    levels = np.array([10, -10, 5, -5, 0])
    if k % 512:
        return np.exp2(np.random.permutation(np.resize(levels, k // 32))).repeat(32)
    a = np.empty((k // 512, 16))
    for p in range(k // 512):
        a[p, :8] = np.random.permutation(np.resize(levels, 8))
        for g in range(8):
            far = levels[np.abs(levels - a[p, g]) >= 10]
            a[p, g + 8] = far[np.random.randint(len(far))]
    return np.exp2(a.ravel()).repeat(32)


def f64(x):
    return np.asarray(x).astype(np.float64)


def striped(idx):
    return np.tile(np.asarray(idx).reshape(-1, 16).T, (8, 1)).astype(np.uint16)


def unstriped(offs):
    return offs[:16].T.reshape(-1).astype(np.int64)


def striped8(idx):
    return np.asarray(idx).reshape(8, -1, 16).transpose(0, 2, 1).reshape(128, -1).astype(np.uint16)


def unstriped8(offs):
    return offs.reshape(8, 16, -1).transpose(0, 2, 1).reshape(8, -1).astype(np.int64)


def pick8(x, idx, run):
    r = np.arange(len(x))
    return x[r[:, None], idx[r % (8 * run) // run]]


E2M1 = np.array([0.0, 0.5, 1.0, 1.5, 2.0, 3.0, 4.0, 6.0, -0.0, -0.5, -1.0, -1.5, -2.0, -3.0, -4.0, -6.0])


def pack_weight(w, fmt):
    k, n = w.shape
    w = f64(np.asarray(w, np.float32).astype(ml_dtypes.bfloat16)).reshape(k // 32, 32, n)
    amax = np.abs(w).max(1)
    if fmt == "e4m3":
        byte = np.frexp(amax)[1] - 1 + 127 - 7
    else:
        mant, ex = np.frexp(amax / 6.0)
        byte = np.where(mant > 0.5, ex, ex - 1) + 127
    byte = np.clip(np.where(amax > 0, byte, 1), 1, 254)
    scaled = (w * np.exp2(127.0 - byte)[:, None, :]).reshape(k, n).astype(np.float32)
    by_word = np.ascontiguousarray(scaled.reshape(k // 512, 128, 4, n).transpose(0, 1, 3, 2))
    if fmt == "e4m3":
        words = by_word.astype(ml_dtypes.float8_e4m3fn).view(np.uint8)
    else:
        c = by_word.astype(ml_dtypes.float4_e2m1fn).view(np.uint8) & 0xF
        words = (c[..., 0::2] | (c[..., 1::2] << 4)).reshape(k // 512, 128, 2 * n)
    return np.ascontiguousarray(words), np.ascontiguousarray(byte.astype(np.uint8).reshape(k // 512, 16, n))


def unpack_weight(words, scales, fmt):
    g, _, n = scales.shape
    words = np.ascontiguousarray(words).reshape(g, 128, n, -1)
    if fmt == "e4m3":
        vals = words.view(ml_dtypes.float8_e4m3fn).astype(np.float64)
    else:
        nib = np.empty((g, 128, n, 4), np.uint8)
        nib[..., 0::2] = words & 0xF
        nib[..., 1::2] = words >> 4
        vals = E2M1[nib]
    vals = vals * np.repeat(np.exp2(scales.astype(np.float64) - 127.0), 8, axis=1)[..., None]
    return vals.transpose(0, 1, 3, 2).reshape(g * 512, n)


K, R, F, T, J, M = 512, 128, 512, 2048, 512, 256


def setup_inputs():
    n = np.random.standard_normal
    idx = np.random.permutation(T)[:J]
    idx2 = np.stack([np.random.permutation(J)[:M] for _ in range(8)])
    idx3 = np.stack([np.random.permutation(J)[:M] for _ in range(8)])
    fk = mx_kscale(K)
    ff = mx_kscale(F)
    tabp = pack_weight(n((K, T)) / fk[:, None], "e2m1")
    dtabp = pack_weight(n((K, T)) / fk[:, None], "e2m1")
    return {
        "tab_words": tabp[0],
        "tab_scales": tabp[1],
        "w1": (n((K, R)) * 1 / np.sqrt(K) * fk[:, None]).astype(np.float32),
        "sharp": (np.random.uniform(0.1, 0.5, (1, M))).astype(np.float32),
        "wo": (n((F, R)) * 1 / np.sqrt(F) * ff[:, None]).astype(np.float32),
        "dy": (n((F, M)) / ff[:, None]).astype(np.float32),
        "dtab_words": dtabp[0],
        "dtab_scales": dtabp[1],
        "og": (np.random.uniform(0.7, 2.0, (R, 1))).astype(np.float32),
        "base": (0.3 * n((R, J))).astype(np.float32),
        "offs": striped(idx),
        "offs2": striped8(idx2),
        "offs3": striped8(idx3),
    }


def reference(tab_words, tab_scales, w1, sharp, wo, dy, dtab_words, dtab_scales, og, base, offs, offs2, offs3):
    idx = unstriped(offs)
    idx2 = unstriped8(offs2)
    idx3 = unstriped8(offs3)
    tabu = unpack_weight(tab_words, tab_scales, "e2m1")
    dtabu = unpack_weight(dtab_words, dtab_scales, "e2m1")
    w1q = mxq(f64(w1), 0, "e4m3")
    tabidxg = tabu[:, idx]
    a = w1q.T @ tabidxg
    dtabidxg = dtabu[:, idx]
    ta = w1q.T @ dtabidxg
    dl = pick8(a, idx2, 16) - pick8(a, idx3, 16)
    u1 = np.exp(np.square(dl) * f64(sharp) * (-1.0))
    woq = mxq(f64(wo), 0, "e4m3")
    dyq = mxq(f64(dy), 0, "e4m3")
    c0 = woq.T @ dyq
    xdl = pick8(ta, idx2, 16) - pick8(ta, idx3, 16)
    xu1 = xdl * dl * 2.0 * f64(sharp) * (-1.0) * u1
    xddl = (xu1 * c0 * (-1.0) * f64(sharp) * dl + xdl * c0 * u1 * (-1.0) * f64(sharp)) * 2.0
    xs1 = np.zeros((R, J))
    xs1[np.arange(R)[:, None], idx2[np.arange(R) % 128 // 16]] = xddl
    xe2 = xddl * (-1.0)
    xs2 = np.zeros((R, J))
    xs2[np.arange(R)[:, None], idx3[np.arange(R) % 128 // 16]] = xe2
    xda = xs1 + xs2
    y = xda * f64(og) + f64(base)
    return y

@@ -1,0 +1,223 @@
+from contextlib import ExitStack
+
+import concourse.mybir as mybir
+from concourse.masks import make_identity
+
+K, R, F, T, J, M = 512, 128, 512, 2048, 512, 256
+FLOPS = 2 * K * R * J * 2 + 2 * F * R * M
+
+F32 = mybir.dt.float32
+BF16 = mybir.dt.bfloat16
+I32 = mybir.dt.int32
+U32 = mybir.dt.uint32
+U16 = mybir.dt.uint16
+U8 = mybir.dt.uint8
+FP8X4 = mybir.dt.float8_e4m3fn_x4
+FP4X4 = mybir.dt.float4_e2m1fn_x4
+ALU = mybir.AluOpType
+ACT = mybir.ActivationFunctionType
+
+P = 128
+PACK = 4
+
+
+def tile_attend_hvpairnear_kernel(
+    tc, tab_words, tab_scales, w1, sharp, wo, dy, dtab_words, dtab_scales, og, base, offs, offs2, offs3, out
+):
+    nc = tc.nc
+    with ExitStack() as ctx:
+        sb = ctx.enter_context(tc.tile_pool(name="sb", bufs=1))
+        ps = ctx.enter_context(tc.psum_pool(name="ps", bufs=1))
+
+        def tile(name, shape, dtype, tag=None):
+            return sb.tile(shape, dtype, name=name, tag=tag or name, align_bytes=64)
+
+        slots = tile("slots", [P, J // 16], U16)
+        left = tile("left", [P, M // 16], U16)
+        right = tile("right", [P, M // 16], U16)
+        words = [tile("words%d" % i, [P, T], U16) for i in range(2)]
+        scales = [tile("scales%d" % i, [P, T], U8) for i in range(2)]
+        w1_raw = tile("w1_raw", [P, PACK, R], F32)
+        wo_raw = tile("wo_raw", [P, PACK, R], F32)
+        dy_raw = tile("dy_raw", [P, PACK, M], F32)
+        sharp_col = tile("sharp_col", [P, 2], F32)
+        og_sb = tile("og_sb", [P, 1], F32)
+        base_sb = tile("base_sb", [P, J], F32)
+        placed = [tile("placed%d" % i, [P, J], F32) for i in range(2)]
+        warm = tile("warm", [P, 1], F32)
+        ident = tile("ident", [P, P], F32)
+
+        for i in range(2):
+            nc.vector.memset(scales[i][:].bitcast(I32), 0)
+        nc.vector.memset(warm[:], 0.0)
+        nc.scalar.activation(warm[:], warm[:], ACT.Exp)
+        for i in range(2):
+            nc.vector.memset(placed[i][:], 0.0)
+        make_identity(nc, ident[:])
+
+        def load_scales(i, src):
+            for q in range(4):
+                nc.sync.dma_start(
+                    out=scales[i][32 * q : 32 * q + 4, :].bitcast(I32), in_=src[0, 4 * q : 4 * q + 4, :].bitcast(I32)
+                )
+
+        def rows(src):
+            return src.rearrange("(p t) c -> p t c", t=PACK)
+
+        nc.sync.dma_start(slots[:], offs)
+        nc.sync.dma_start(out=words[0][:].bitcast(I32), in_=tab_words[0].bitcast(I32))
+        load_scales(0, tab_scales)
+        nc.sync.dma_start(out=w1_raw[:], in_=rows(w1))
+        nc.sync.dma_start(out=wo_raw[:], in_=rows(wo))
+        nc.sync.dma_start(out=words[1][:].bitcast(I32), in_=dtab_words[0].bitcast(I32))
+        nc.sync.dma_start(right[:], offs3)
+        nc.sync.dma_start(left[:], offs2)
+        nc.sync.dma_start(out=dy_raw[:], in_=rows(dy))
+        with nc.allow_non_contiguous_dma(reason="one sharpness value to a partition"):
+            nc.sync.dma_start(out=sharp_col[:], in_=sharp.rearrange("o (h p) -> p (o h)", p=P))
+        load_scales(1, dtab_scales)
+        nc.sync.dma_start(out=og_sb[:], in_=og)
+        nc.sync.dma_start(out=base_sb[:], in_=base)
+
+        def interleave(name, raw, width):
+            grouped = tile(name + "_bf", [P, width, PACK], BF16)
+            nc.scalar.copy(
+                grouped[:].rearrange("p (c i) t -> p c t i", i=4), raw[:].rearrange("p t (c i) -> p c t i", i=4)
+            )
+            return grouped
+
+        def quantize(name, grouped, width):
+            codes = tile(name + "_codes", [P, width], U32)
+            plane = tile(name + "_plane", [P, width], U8)
+            nc.vector.quantize_mx(
+                out=codes[:].bitcast(FP8X4), scales=plane[:], in_=grouped[:].rearrange("p c t -> p (c t)")
+            )
+            return codes, plane
+
+        def gather(name, window, dtype):
+            got = tile(name, [P, J], dtype)
+            nc.vector.tensor_copy(got[:], window[:].indirect(slots[:]))
+            return got
+
+        def product(name, got_words, got_scales, g):
+            cols = slice(g * J // 2, (g + 1) * J // 2)
+            bank = ps.tile([P, J // 2], F32, name=name)
+            nc.tensor.matmul_mx(
+                out=bank[:],
+                lhsT=w1_codes[:].bitcast(FP8X4),
+                lhsT_scale=w1_plane[:],
+                rhs=got_words[:, cols].bitcast(FP4X4),
+                rhs_scale=got_scales[:, cols],
+                start=True,
+                stop=True,
+            )
+            return bank
+
+        def half(h):
+            return slice(h * P, (h + 1) * P)
+
+        w1_bf = interleave("w1", w1_raw, R)
+        tab_w = gather("tab_w", words[0], U16)
+        tab_s = gather("tab_s", scales[0], U8)
+        w1_codes, w1_plane = quantize("w1", w1_bf, R)
+        wo_bf = interleave("wo", wo_raw, R)
+        a = tile("a", [P, J], F32)
+        for g in range(2):
+            a_bank = product("a_bank%d" % g, tab_w, tab_s, g)
+            nc.scalar.copy(a[:, g * J // 2 : (g + 1) * J // 2], a_bank[:])
+        dtab_w = gather("dtab_w", words[1], U16)
+        wo_codes, wo_plane = quantize("wo", wo_bf, R)
+        dy_bf = interleave("dy", dy_raw, M)
+
+        a_right = tile("a_right", [P, M], F32)
+        nc.vector.tensor_scalar(a_right[:], a[:].indirect(right[:]), -1.0, 0.0, ALU.mult, ALU.add)
+        a_left = tile("a_left", [P, M], F32)
+        nc.vector.tensor_copy(a_left[:], a[:].indirect(left[:]))
+        dl_t = ps.tile([P, M], F32, name="dl_t")
+        for i, side in enumerate((a_right, a_left)):
+            for h in range(2):
+                nc.tensor.matmul(
+                    dl_t[:, half(h)], side[:, half(h)], ident[:], start=(i + h == 0), stop=(i + h == 2), is_transpose=True
+                )
+
+        dtab_s = tile("dtab_s", [P, J], U8, tag="a_right")
+        ta_banks = []
+        for g in range(2):
+            nc.vector.tensor_copy(
+                dtab_s[:, g * J // 2 : (g + 1) * J // 2], scales[1][:].indirect(slots[:, g * J // 32 : (g + 1) * J // 32])
+            )
+            ta_banks.append(product("ta_bank%d" % g, dtab_w, dtab_s, g))
+        dy_codes, dy_plane = quantize("dy", dy_bf, M)
+        c0_t = ps.tile([P, M], F32, name="c0_t")
+        for h in range(2):
+            nc.tensor.matmul_mx(
+                out=c0_t[:, half(h)],
+                lhsT=dy_codes[:, half(h)].bitcast(FP8X4),
+                lhsT_scale=dy_plane[:, half(h)],
+                rhs=wo_codes[:].bitcast(FP8X4),
+                rhs_scale=wo_plane[:],
+                start=True,
+                stop=True,
+            )
+
+        decay = tile("decay", [P, 2], F32)
+        slope = tile("slope", [P, 2], F32)
+        shift = tile("shift", [P, 2], F32)
+        nc.scalar.activation(decay[:], sharp_col[:], ACT.Copy, scale=-1.0)
+        nc.scalar.activation(slope[:], sharp_col[:], ACT.Square, scale=2.0)
+        nc.scalar.activation(shift[:], sharp_col[:], ACT.Copy, scale=-2.0)
+
+        sq_t = tile("sq_t", [P, M], F32, tag="dy_raw")
+        nc.scalar.activation(sq_t[:], dl_t[:], ACT.Square)
+        u_t = tile("u_t", [P, M], F32)
+        bend_t = tile("bend_t", [P, M], F32)
+        for h in range(2):
+            nc.scalar.activation(u_t[:, half(h)], sq_t[:, half(h)], ACT.Exp, scale=decay[:, h : h + 1])
+        for h in range(2):
+            nc.scalar.activation(
+                bend_t[:, half(h)], sq_t[:, half(h)], ACT.Identity, scale=slope[:, h : h + 1], bias=shift[:, h : h + 1]
+            )
+        ta = tile("ta", [P, J], F32, tag="dy_raw")
+        for g in range(2):
+            nc.scalar.copy(ta[:, g * J // 2 : (g + 1) * J // 2], ta_banks[g][:])
+
+        scratch = tile("scratch", [P, M], F32, tag="scales1")
+        nc.vector.tensor_tensor(scratch[:], u_t[:], bend_t[:], ALU.mult)
+        weight_t = tile("weight_t", [P, M], F32)
+        nc.vector.tensor_tensor(weight_t[:], c0_t[:], scratch[:], ALU.mult)
+        weight_bank = ps.tile([P, M], F32, name="dl_t")
+        for h in range(2):
+            nc.tensor.transpose(weight_bank[:, half(h)], weight_t[:, half(h)], ident[:])
+        weight = tile("weight", [P, M], F32)
+        nc.scalar.activation(weight[:], weight_bank[:], ACT.Copy, scale=og_sb[:])
+
+        ta_right = tile("ta_right", [P, M], F32)
+        nc.vector.tensor_copy(ta_right[:], ta[:].indirect(right[:]))
+        xdl = tile("xdl", [P, M], F32)
+        nc.vector.tensor_tensor(xdl[:], ta[:].indirect(left[:]), ta_right[:], ALU.subtract)
+
+        sum_t = [ps.tile([P, 2 * P], F32, name="sum_t%d" % g) for g in range(2)]
+        for g in range(2):
+            for h in range(2):
+                nc.tensor.matmul(
+                    sum_t[g][:, half(h)], base_sb[:, half(2 * g + h)], ident[:], start=(h == 0), stop=False, is_transpose=True
+                )
+
+        nc.vector.tensor_tensor(placed[0][:].indirect(left[:]), weight[:], xdl[:], ALU.mult)
+        nc.vector.tensor_tensor(placed[1][:].indirect(right[:]), weight[:], xdl[:], ALU.mult)
+
+        for g in range(2):
+            for h in range(2):
+                nc.tensor.matmul(
+                    sum_t[g][:, half(h)], placed[0][:, half(2 * g + h)], ident[:], start=False, stop=(h == 1), is_transpose=True
+                )
+        for g in range(2):
+            cols = slice(g * 2 * P, (g + 1) * 2 * P)
+            turned = tile("turned%d" % g, [P, 2 * P], F32)
+            nc.scalar.copy(turned[:], sum_t[g][:])
+            partial = ps.tile([P, J // 2], F32, name="a_bank%d" % g)
+            for h in range(2):
+                nc.tensor.transpose(partial[:, half(h)], turned[:, half(h)], ident[:])
+            result = tile("result%d" % g, [P, 2 * P], F32)
+            nc.vector.tensor_tensor(result[:], partial[:], placed[1][:, cols], ALU.subtract)
+            nc.sync.dma_start(out=out[:, cols], in_=result[:])

@@ -56,10 +56,8 @@ def tile_attend_hvpairnear_kernel(
         make_identity(nc, ident[:])
 
         def load_scales(i, src):
-            for q in range(4):
-                nc.sync.dma_start(
-                    out=scales[i][32 * q : 32 * q + 4, :].bitcast(I32), in_=src[0, 4 * q : 4 * q + 4, :].bitcast(I32)
-                )
+            for r in range(4):
+                nc.sync.dma_start(out=scales[i][r:P:32, :].bitcast(I32), in_=src[0, r:16:4, :].bitcast(I32))
 
         def rows(src):
             return src.rearrange("(p t) c -> p t c", t=PACK)
@@ -68,14 +66,14 @@ def tile_attend_hvpairnear_kernel(
         nc.sync.dma_start(out=words[0][:].bitcast(I32), in_=tab_words[0].bitcast(I32))
         load_scales(0, tab_scales)
         nc.sync.dma_start(out=w1_raw[:], in_=rows(w1))
-        nc.sync.dma_start(out=wo_raw[:], in_=rows(wo))
-        nc.sync.dma_start(out=words[1][:].bitcast(I32), in_=dtab_words[0].bitcast(I32))
         nc.sync.dma_start(right[:], offs3)
+        nc.sync.dma_start(out=words[1][:].bitcast(I32), in_=dtab_words[0].bitcast(I32))
         nc.sync.dma_start(left[:], offs2)
         nc.sync.dma_start(out=dy_raw[:], in_=rows(dy))
+        nc.sync.dma_start(out=wo_raw[:], in_=rows(wo))
+        load_scales(1, dtab_scales)
         with nc.allow_non_contiguous_dma(reason="one sharpness value to a partition"):
             nc.sync.dma_start(out=sharp_col[:], in_=sharp.rearrange("o (h p) -> p (o h)", p=P))
-        load_scales(1, dtab_scales)
         nc.sync.dma_start(out=og_sb[:], in_=og)
         nc.sync.dma_start(out=base_sb[:], in_=base)
 
@@ -86,8 +84,8 @@ def tile_attend_hvpairnear_kernel(
             )
             return grouped
 
-        def quantize(name, grouped, width):
-            codes = tile(name + "_codes", [P, width], U32)
+        def quantize(name, grouped, width, tag=None):
+            codes = tile(name + "_codes", [P, width], U32, tag=tag)
             plane = tile(name + "_plane", [P, width], U8)
             nc.vector.quantize_mx(
                 out=codes[:].bitcast(FP8X4), scales=plane[:], in_=grouped[:].rearrange("p c t -> p (c t)")
@@ -99,7 +97,7 @@ def tile_attend_hvpairnear_kernel(
             nc.vector.tensor_copy(got[:], window[:].indirect(slots[:]))
             return got
 
-        def product(name, got_words, got_scales, g):
+        def product(name, got_words, plane, g):
             cols = slice(g * J // 2, (g + 1) * J // 2)
             bank = ps.tile([P, J // 2], F32, name=name)
             nc.tensor.matmul_mx(
@@ -107,7 +105,7 @@ def tile_attend_hvpairnear_kernel(
                 lhsT=w1_codes[:].bitcast(FP8X4),
                 lhsT_scale=w1_plane[:],
                 rhs=got_words[:, cols].bitcast(FP4X4),
-                rhs_scale=got_scales[:, cols],
+                rhs_scale=plane,
                 start=True,
                 stop=True,
             )
@@ -120,14 +118,13 @@ def tile_attend_hvpairnear_kernel(
         tab_w = gather("tab_w", words[0], U16)
         tab_s = gather("tab_s", scales[0], U8)
         w1_codes, w1_plane = quantize("w1", w1_bf, R)
-        wo_bf = interleave("wo", wo_raw, R)
         a = tile("a", [P, J], F32)
         for g in range(2):
-            a_bank = product("a_bank%d" % g, tab_w, tab_s, g)
+            a_bank = product("a_bank%d" % g, tab_w, tab_s[:, g * J // 2 : (g + 1) * J // 2], g)
             nc.scalar.copy(a[:, g * J // 2 : (g + 1) * J // 2], a_bank[:])
         dtab_w = gather("dtab_w", words[1], U16)
-        wo_codes, wo_plane = quantize("wo", wo_bf, R)
         dy_bf = interleave("dy", dy_raw, M)
+        wo_bf = interleave("wo", wo_raw, R)
 
         a_right = tile("a_right", [P, M], F32)
         nc.vector.tensor_scalar(a_right[:], a[:].indirect(right[:]), -1.0, 0.0, ALU.mult, ALU.add)
@@ -140,14 +137,13 @@ def tile_attend_hvpairnear_kernel(
                     dl_t[:, half(h)], side[:, half(h)], ident[:], start=(i + h == 0), stop=(i + h == 2), is_transpose=True
                 )
 
-        dtab_s = tile("dtab_s", [P, J], U8, tag="a_right")
+        dy_codes, dy_plane = quantize("dy", dy_bf, M)
         ta_banks = []
         for g in range(2):
-            nc.vector.tensor_copy(
-                dtab_s[:, g * J // 2 : (g + 1) * J // 2], scales[1][:].indirect(slots[:, g * J // 32 : (g + 1) * J // 32])
-            )
-            ta_banks.append(product("ta_bank%d" % g, dtab_w, dtab_s, g))
-        dy_codes, dy_plane = quantize("dy", dy_bf, M)
+            dtab_s = tile("dtab_s%d" % g, [P, J // 2], U8, tag=("a_right", None)[g])
+            nc.vector.tensor_copy(dtab_s[:], scales[1][:].indirect(slots[:, g * J // 32 : (g + 1) * J // 32]))
+            ta_banks.append(product("ta_bank%d" % g, dtab_w, dtab_s[:], g))
+        wo_codes, wo_plane = quantize("wo", wo_bf, R, tag="a_right")
         c0_t = ps.tile([P, M], F32, name="c0_t")
         for h in range(2):
             nc.tensor.matmul_mx(
@@ -167,7 +163,7 @@ def tile_attend_hvpairnear_kernel(
         nc.scalar.activation(slope[:], sharp_col[:], ACT.Square, scale=2.0)
         nc.scalar.activation(shift[:], sharp_col[:], ACT.Copy, scale=-2.0)
 
-        sq_t = tile("sq_t", [P, M], F32, tag="dy_raw")
+        sq_t = tile("sq_t", [P, M], F32, tag="wo_raw")
         nc.scalar.activation(sq_t[:], dl_t[:], ACT.Square)
         u_t = tile("u_t", [P, M], F32)
         bend_t = tile("bend_t", [P, M], F32)
@@ -177,11 +173,11 @@ def tile_attend_hvpairnear_kernel(
             nc.scalar.activation(
                 bend_t[:, half(h)], sq_t[:, half(h)], ACT.Identity, scale=slope[:, h : h + 1], bias=shift[:, h : h + 1]
             )
-        ta = tile("ta", [P, J], F32, tag="dy_raw")
+        ta = tile("ta", [P, J], F32, tag="wo_raw")
         for g in range(2):
             nc.scalar.copy(ta[:, g * J // 2 : (g + 1) * J // 2], ta_banks[g][:])
 
-        scratch = tile("scratch", [P, M], F32, tag="scales1")
+        scratch = tile("scratch", [P, M], F32, tag="wo_bf")
         nc.vector.tensor_tensor(scratch[:], u_t[:], bend_t[:], ALU.mult)
         weight_t = tile("weight_t", [P, M], F32)
         nc.vector.tensor_tensor(weight_t[:], c0_t[:], scratch[:], ALU.mult)

@@ -1,3 +1,4 @@
+import math
 from contextlib import ExitStack
 
 import concourse.mybir as mybir
@@ -66,14 +67,14 @@ def tile_attend_hvpairnear_kernel(
         nc.sync.dma_start(out=words[0][:].bitcast(I32), in_=tab_words[0].bitcast(I32))
         load_scales(0, tab_scales)
         nc.sync.dma_start(out=w1_raw[:], in_=rows(w1))
-        nc.sync.dma_start(right[:], offs3)
+        nc.sync.dma_start(out=wo_raw[:], in_=rows(wo))
         nc.sync.dma_start(out=words[1][:].bitcast(I32), in_=dtab_words[0].bitcast(I32))
+        nc.sync.dma_start(right[:], offs3)
         nc.sync.dma_start(left[:], offs2)
         nc.sync.dma_start(out=dy_raw[:], in_=rows(dy))
-        nc.sync.dma_start(out=wo_raw[:], in_=rows(wo))
-        load_scales(1, dtab_scales)
         with nc.allow_non_contiguous_dma(reason="one sharpness value to a partition"):
             nc.sync.dma_start(out=sharp_col[:], in_=sharp.rearrange("o (h p) -> p (o h)", p=P))
+        load_scales(1, dtab_scales)
         nc.sync.dma_start(out=og_sb[:], in_=og)
         nc.sync.dma_start(out=base_sb[:], in_=base)
 
@@ -84,8 +85,8 @@ def tile_attend_hvpairnear_kernel(
             )
             return grouped
 
-        def quantize(name, grouped, width, tag=None):
-            codes = tile(name + "_codes", [P, width], U32, tag=tag)
+        def quantize(name, grouped, width):
+            codes = tile(name + "_codes", [P, width], U32)
             plane = tile(name + "_plane", [P, width], U8)
             nc.vector.quantize_mx(
                 out=codes[:].bitcast(FP8X4), scales=plane[:], in_=grouped[:].rearrange("p c t -> p (c t)")
@@ -118,32 +119,32 @@ def tile_attend_hvpairnear_kernel(
         tab_w = gather("tab_w", words[0], U16)
         tab_s = gather("tab_s", scales[0], U8)
         w1_codes, w1_plane = quantize("w1", w1_bf, R)
+        wo_bf = interleave("wo", wo_raw, R)
         a = tile("a", [P, J], F32)
         for g in range(2):
             a_bank = product("a_bank%d" % g, tab_w, tab_s[:, g * J // 2 : (g + 1) * J // 2], g)
             nc.scalar.copy(a[:, g * J // 2 : (g + 1) * J // 2], a_bank[:])
         dtab_w = gather("dtab_w", words[1], U16)
+        wo_codes, wo_plane = quantize("wo", wo_bf, R)
         dy_bf = interleave("dy", dy_raw, M)
-        wo_bf = interleave("wo", wo_raw, R)
 
         a_right = tile("a_right", [P, M], F32)
         nc.vector.tensor_scalar(a_right[:], a[:].indirect(right[:]), -1.0, 0.0, ALU.mult, ALU.add)
-        a_left = tile("a_left", [P, M], F32)
-        nc.vector.tensor_copy(a_left[:], a[:].indirect(left[:]))
-        dl_t = ps.tile([P, M], F32, name="dl_t")
-        for i, side in enumerate((a_right, a_left)):
-            for h in range(2):
-                nc.tensor.matmul(
-                    dl_t[:, half(h)], side[:, half(h)], ident[:], start=(i + h == 0), stop=(i + h == 2), is_transpose=True
-                )
+        dl_t = []
+        for h in range(2):
+            a_left = tile("a_left%d" % h, [P, P], F32)
+            nc.vector.tensor_copy(a_left[:], a[:].indirect(left[:, h * P // 16 : (h + 1) * P // 16]))
+            bank = ps.tile([P, P], F32, name="dl_t%d" % h)
+            nc.tensor.matmul(bank[:], a_right[:, half(h)], ident[:], start=True, stop=False, is_transpose=True)
+            nc.tensor.matmul(bank[:], a_left[:], ident[:], start=False, stop=True, is_transpose=True)
+            dl_t.append(bank)
 
-        dy_codes, dy_plane = quantize("dy", dy_bf, M)
         ta_banks = []
         for g in range(2):
             dtab_s = tile("dtab_s%d" % g, [P, J // 2], U8, tag=("a_right", None)[g])
             nc.vector.tensor_copy(dtab_s[:], scales[1][:].indirect(slots[:, g * J // 32 : (g + 1) * J // 32]))
-            ta_banks.append(product("ta_bank%d" % g, dtab_w, dtab_s[:], g))
-        wo_codes, wo_plane = quantize("wo", wo_bf, R, tag="a_right")
+            ta_banks.append(product("a_bank%d" % g, dtab_w, dtab_s[:], g))
+        dy_codes, dy_plane = quantize("dy", dy_bf, M)
         c0_t = ps.tile([P, M], F32, name="c0_t")
         for h in range(2):
             nc.tensor.matmul_mx(
@@ -156,32 +157,31 @@ def tile_attend_hvpairnear_kernel(
                 stop=True,
             )
 
-        decay = tile("decay", [P, 2], F32)
         slope = tile("slope", [P, 2], F32)
         shift = tile("shift", [P, 2], F32)
-        nc.scalar.activation(decay[:], sharp_col[:], ACT.Copy, scale=-1.0)
-        nc.scalar.activation(slope[:], sharp_col[:], ACT.Square, scale=2.0)
+        nc.scalar.activation(slope[:], sharp_col[:], ACT.Square, scale=math.sqrt(8.0))
         nc.scalar.activation(shift[:], sharp_col[:], ACT.Copy, scale=-2.0)
 
-        sq_t = tile("sq_t", [P, M], F32, tag="wo_raw")
-        nc.scalar.activation(sq_t[:], dl_t[:], ACT.Square)
         u_t = tile("u_t", [P, M], F32)
         bend_t = tile("bend_t", [P, M], F32)
+        sq_t = tile("sq_t", [P, M], F32, tag="dy_raw")
         for h in range(2):
-            nc.scalar.activation(u_t[:, half(h)], sq_t[:, half(h)], ACT.Exp, scale=decay[:, h : h + 1])
+            nc.scalar.activation(sq_t[:, half(h)], dl_t[h][:], ACT.Square, scale=math.sqrt(0.5))
         for h in range(2):
             nc.scalar.activation(
                 bend_t[:, half(h)], sq_t[:, half(h)], ACT.Identity, scale=slope[:, h : h + 1], bias=shift[:, h : h + 1]
             )
-        ta = tile("ta", [P, J], F32, tag="wo_raw")
+        for h in range(2):
+            nc.scalar.activation(u_t[:, half(h)], sq_t[:, half(h)], ACT.Exp, scale=shift[:, h : h + 1])
+        ta = tile("ta", [P, J], F32, tag="slope")
         for g in range(2):
             nc.scalar.copy(ta[:, g * J // 2 : (g + 1) * J // 2], ta_banks[g][:])
 
-        scratch = tile("scratch", [P, M], F32, tag="wo_bf")
+        scratch = tile("scratch", [P, M], F32, tag="a_right")
         nc.vector.tensor_tensor(scratch[:], u_t[:], bend_t[:], ALU.mult)
         weight_t = tile("weight_t", [P, M], F32)
         nc.vector.tensor_tensor(weight_t[:], c0_t[:], scratch[:], ALU.mult)
-        weight_bank = ps.tile([P, M], F32, name="dl_t")
+        weight_bank = ps.tile([P, M], F32, name="dl_t0")
         for h in range(2):
             nc.tensor.transpose(weight_bank[:, half(h)], weight_t[:, half(h)], ident[:])
         weight = tile("weight", [P, M], F32)

import math
from contextlib import ExitStack

import concourse.mybir as mybir
from concourse.masks import make_identity

K, R, F, T, J, M = 512, 128, 512, 2048, 512, 256
FLOPS = 2 * K * R * J * 2 + 2 * F * R * M

F32 = mybir.dt.float32
BF16 = mybir.dt.bfloat16
I32 = mybir.dt.int32
U32 = mybir.dt.uint32
U16 = mybir.dt.uint16
U8 = mybir.dt.uint8
FP8X4 = mybir.dt.float8_e4m3fn_x4
FP4X4 = mybir.dt.float4_e2m1fn_x4
ALU = mybir.AluOpType
ACT = mybir.ActivationFunctionType

P = 128
PACK = 4


def tile_attend_hvpairnear_kernel(
    tc, tab_words, tab_scales, w1, sharp, wo, dy, dtab_words, dtab_scales, og, base, offs, offs2, offs3, out
):
    nc = tc.nc
    with ExitStack() as ctx:
        sb = ctx.enter_context(tc.tile_pool(name="sb", bufs=1))
        ps = ctx.enter_context(tc.psum_pool(name="ps", bufs=1))

        def tile(name, shape, dtype, tag=None):
            return sb.tile(shape, dtype, name=name, tag=tag or name, align_bytes=64)

        slots = tile("slots", [P, J // 16], U16)
        left = tile("left", [P, M // 16], U16)
        right = tile("right", [P, M // 16], U16)
        words = [tile("words%d" % i, [P, T], U16) for i in range(2)]
        scales = [tile("scales%d" % i, [P, T], U8) for i in range(2)]
        w1_raw = tile("w1_raw", [P, PACK, R], F32)
        wo_raw = tile("wo_raw", [P, PACK, R], F32)
        dy_raw = tile("dy_raw", [P, PACK, M], F32)
        sharp_col = tile("sharp_col", [P, 2], F32)
        og_sb = tile("og_sb", [P, 1], F32)
        base_sb = tile("base_sb", [P, J], F32)
        placed = [tile("placed%d" % i, [P, J], F32) for i in range(2)]
        warm = tile("warm", [P, 1], F32)
        ident = tile("ident", [P, P], F32)

        for i in range(2):
            nc.vector.memset(scales[i][:].bitcast(I32), 0)
        nc.vector.memset(warm[:], 0.0)
        nc.scalar.activation(warm[:], warm[:], ACT.Exp)
        for i in range(2):
            nc.vector.memset(placed[i][:], 0.0)
        make_identity(nc, ident[:])

        def load_scales(i, src):
            for r in range(4):
                nc.sync.dma_start(out=scales[i][r:P:32, :].bitcast(I32), in_=src[0, r:16:4, :].bitcast(I32))

        def rows(src):
            return src.rearrange("(p t) c -> p t c", t=PACK)

        nc.sync.dma_start(slots[:], offs)
        nc.sync.dma_start(out=words[0][:].bitcast(I32), in_=tab_words[0].bitcast(I32))
        load_scales(0, tab_scales)
        nc.sync.dma_start(out=w1_raw[:], in_=rows(w1))
        nc.sync.dma_start(out=wo_raw[:], in_=rows(wo))
        nc.sync.dma_start(out=words[1][:].bitcast(I32), in_=dtab_words[0].bitcast(I32))
        nc.sync.dma_start(right[:], offs3)
        nc.sync.dma_start(left[:], offs2)
        nc.sync.dma_start(out=dy_raw[:], in_=rows(dy))
        with nc.allow_non_contiguous_dma(reason="one sharpness value to a partition"):
            nc.sync.dma_start(out=sharp_col[:], in_=sharp.rearrange("o (h p) -> p (o h)", p=P))
        load_scales(1, dtab_scales)
        nc.sync.dma_start(out=og_sb[:], in_=og)
        nc.sync.dma_start(out=base_sb[:], in_=base)

        def interleave(name, raw, width):
            grouped = tile(name + "_bf", [P, width, PACK], BF16)
            nc.scalar.copy(
                grouped[:].rearrange("p (c i) t -> p c t i", i=4), raw[:].rearrange("p t (c i) -> p c t i", i=4)
            )
            return grouped

        def quantize(name, grouped, width):
            codes = tile(name + "_codes", [P, width], U32)
            plane = tile(name + "_plane", [P, width], U8)
            nc.vector.quantize_mx(
                out=codes[:].bitcast(FP8X4), scales=plane[:], in_=grouped[:].rearrange("p c t -> p (c t)")
            )
            return codes, plane

        def gather(name, window, dtype):
            got = tile(name, [P, J], dtype)
            nc.vector.tensor_copy(got[:], window[:].indirect(slots[:]))
            return got

        def product(name, got_words, plane, g):
            cols = slice(g * J // 2, (g + 1) * J // 2)
            bank = ps.tile([P, J // 2], F32, name=name)
            nc.tensor.matmul_mx(
                out=bank[:],
                lhsT=w1_codes[:].bitcast(FP8X4),
                lhsT_scale=w1_plane[:],
                rhs=got_words[:, cols].bitcast(FP4X4),
                rhs_scale=plane,
                start=True,
                stop=True,
            )
            return bank

        def half(h):
            return slice(h * P, (h + 1) * P)

        w1_bf = interleave("w1", w1_raw, R)
        tab_w = gather("tab_w", words[0], U16)
        tab_s = gather("tab_s", scales[0], U8)
        w1_codes, w1_plane = quantize("w1", w1_bf, R)
        wo_bf = interleave("wo", wo_raw, R)
        a = tile("a", [P, J], F32)
        for g in range(2):
            a_bank = product("a_bank%d" % g, tab_w, tab_s[:, g * J // 2 : (g + 1) * J // 2], g)
            nc.scalar.copy(a[:, g * J // 2 : (g + 1) * J // 2], a_bank[:])
        dtab_w = gather("dtab_w", words[1], U16)
        wo_codes, wo_plane = quantize("wo", wo_bf, R)
        dy_bf = interleave("dy", dy_raw, M)

        a_right = tile("a_right", [P, M], F32)
        nc.vector.tensor_scalar(a_right[:], a[:].indirect(right[:]), -1.0, 0.0, ALU.mult, ALU.add)
        dl_t = []
        for h in range(2):
            a_left = tile("a_left%d" % h, [P, P], F32)
            nc.vector.tensor_copy(a_left[:], a[:].indirect(left[:, h * P // 16 : (h + 1) * P // 16]))
            bank = ps.tile([P, P], F32, name="dl_t%d" % h)
            nc.tensor.matmul(bank[:], a_right[:, half(h)], ident[:], start=True, stop=False, is_transpose=True)
            nc.tensor.matmul(bank[:], a_left[:], ident[:], start=False, stop=True, is_transpose=True)
            dl_t.append(bank)

        ta_banks = []
        for g in range(2):
            dtab_s = tile("dtab_s%d" % g, [P, J // 2], U8, tag=("a_right", None)[g])
            nc.vector.tensor_copy(dtab_s[:], scales[1][:].indirect(slots[:, g * J // 32 : (g + 1) * J // 32]))
            ta_banks.append(product("a_bank%d" % g, dtab_w, dtab_s[:], g))
        dy_codes, dy_plane = quantize("dy", dy_bf, M)
        c0_t = ps.tile([P, M], F32, name="c0_t")
        for h in range(2):
            nc.tensor.matmul_mx(
                out=c0_t[:, half(h)],
                lhsT=dy_codes[:, half(h)].bitcast(FP8X4),
                lhsT_scale=dy_plane[:, half(h)],
                rhs=wo_codes[:].bitcast(FP8X4),
                rhs_scale=wo_plane[:],
                start=True,
                stop=True,
            )

        slope = tile("slope", [P, 2], F32)
        shift = tile("shift", [P, 2], F32)
        nc.scalar.activation(slope[:], sharp_col[:], ACT.Square, scale=math.sqrt(8.0))
        nc.scalar.activation(shift[:], sharp_col[:], ACT.Copy, scale=-2.0)

        u_t = tile("u_t", [P, M], F32)
        bend_t = tile("bend_t", [P, M], F32)
        sq_t = tile("sq_t", [P, M], F32, tag="dy_raw")
        for h in range(2):
            nc.scalar.activation(sq_t[:, half(h)], dl_t[h][:], ACT.Square, scale=math.sqrt(0.5))
        for h in range(2):
            nc.scalar.activation(
                bend_t[:, half(h)], sq_t[:, half(h)], ACT.Identity, scale=slope[:, h : h + 1], bias=shift[:, h : h + 1]
            )
        for h in range(2):
            nc.scalar.activation(u_t[:, half(h)], sq_t[:, half(h)], ACT.Exp, scale=shift[:, h : h + 1])
        ta = tile("ta", [P, J], F32, tag="slope")
        for g in range(2):
            nc.scalar.copy(ta[:, g * J // 2 : (g + 1) * J // 2], ta_banks[g][:])

        scratch = tile("scratch", [P, M], F32, tag="a_right")
        nc.vector.tensor_tensor(scratch[:], u_t[:], bend_t[:], ALU.mult)
        weight_t = tile("weight_t", [P, M], F32)
        nc.vector.tensor_tensor(weight_t[:], c0_t[:], scratch[:], ALU.mult)
        weight_bank = ps.tile([P, M], F32, name="dl_t0")
        for h in range(2):
            nc.tensor.transpose(weight_bank[:, half(h)], weight_t[:, half(h)], ident[:])
        weight = tile("weight", [P, M], F32)
        nc.scalar.activation(weight[:], weight_bank[:], ACT.Copy, scale=og_sb[:])

        ta_right = tile("ta_right", [P, M], F32)
        nc.vector.tensor_copy(ta_right[:], ta[:].indirect(right[:]))
        xdl = tile("xdl", [P, M], F32)
        nc.vector.tensor_tensor(xdl[:], ta[:].indirect(left[:]), ta_right[:], ALU.subtract)

        sum_t = [ps.tile([P, 2 * P], F32, name="sum_t%d" % g) for g in range(2)]
        for g in range(2):
            for h in range(2):
                nc.tensor.matmul(
                    sum_t[g][:, half(h)], base_sb[:, half(2 * g + h)], ident[:], start=(h == 0), stop=False, is_transpose=True
                )

        nc.vector.tensor_tensor(placed[0][:].indirect(left[:]), weight[:], xdl[:], ALU.mult)
        nc.vector.tensor_tensor(placed[1][:].indirect(right[:]), weight[:], xdl[:], ALU.mult)

        for g in range(2):
            for h in range(2):
                nc.tensor.matmul(
                    sum_t[g][:, half(h)], placed[0][:, half(2 * g + h)], ident[:], start=False, stop=(h == 1), is_transpose=True
                )
        for g in range(2):
            cols = slice(g * 2 * P, (g + 1) * 2 * P)
            turned = tile("turned%d" % g, [P, 2 * P], F32)
            nc.scalar.copy(turned[:], sum_t[g][:])
            partial = ps.tile([P, J // 2], F32, name="a_bank%d" % g)
            for h in range(2):
                nc.tensor.transpose(partial[:, half(h)], turned[:, half(h)], ident[:])
            result = tile("result%d" % g, [P, 2 * P], F32)
            nc.vector.tensor_tensor(result[:], partial[:], placed[1][:, cols], ALU.subtract)
            nc.sync.dma_start(out=out[:, cols], in_=result[:])
